import numpy as np
import ml_dtypes


def mxq(x, axis, fmt="e4m3"):
    dtype, down = {"e4m3": (ml_dtypes.float8_e4m3fn, 7), "e5m2": (ml_dtypes.float8_e5m2, 14)}[fmt]
    v = np.moveaxis(np.asarray(x, np.float32).astype(ml_dtypes.bfloat16).astype(np.float64), axis, -1)
    blocks = v.reshape(v.shape[:-1] + (-1, 32))
    amax = np.abs(blocks).max(-1, keepdims=True)
    byte = np.maximum(np.where(amax > 0, np.frexp(amax)[1] - 1 + 127, 0) - down, 1)
    scale = np.exp2(byte - 127.0)
    codes = (blocks / scale).astype(np.float32).astype(dtype).astype(np.float64)
    return np.moveaxis((codes * scale).reshape(v.shape), -1, axis)


WIDE = False


def mx_kscale(k):
    if not WIDE:
        return np.ones(k)
    levels = np.array([10, -10, 5, -5, 0])
    if k % 512:
        return np.exp2(np.random.permutation(np.resize(levels, k // 32))).repeat(32)
    a = np.empty((k // 512, 16))
    for p in range(k // 512):
        a[p, :8] = np.random.permutation(np.resize(levels, 8))
        for g in range(8):
            far = levels[np.abs(levels - a[p, g]) >= 10]
            a[p, g + 8] = far[np.random.randint(len(far))]
    return np.exp2(a.ravel()).repeat(32)


def f64(x):
    return np.asarray(x).astype(np.float64)


def striped(idx):
    return np.tile(idx.reshape(-1, 16).T, (8, 1)).astype(np.uint16)


def unstriped(offs):
    return offs[:16].T.reshape(-1).astype(np.int64)


def pack_weight(w):
    k, n = w.shape
    w = f64(np.asarray(w, np.float32).astype(ml_dtypes.bfloat16)).reshape(k // 32, 32, n)
    amax = np.abs(w).max(1)
    byte = np.clip(np.where(amax > 0, np.frexp(amax)[1] - 1 + 127 - 7, 1), 1, 254)
    scaled = (w * np.exp2(127.0 - byte)[:, None, :]).reshape(k, n).astype(np.float32)
    words = np.ascontiguousarray(scaled.reshape(k // 512, 128, 4, n).transpose(0, 1, 3, 2)).astype(ml_dtypes.float8_e4m3fn).view(np.uint8)
    return words, np.ascontiguousarray(byte.astype(np.uint8).reshape(k // 512, 16, n))


def unpack_weight(words, scales):
    g, p, n, _ = words.shape
    vals = np.ascontiguousarray(words).view(ml_dtypes.float8_e4m3fn).astype(np.float64) * np.repeat(np.exp2(scales.astype(np.float64) - 127.0), 8, axis=1)[..., None]
    return vals.transpose(0, 1, 3, 2).reshape(g * 512, n)


E2M1 = np.array([0.0, 0.5, 1.0, 1.5, 2.0, 3.0, 4.0, 6.0, -0.0, -0.5, -1.0, -1.5, -2.0, -3.0, -4.0, -6.0])


def pack_fp4(w):
    k, n = w.shape
    w = f64(np.asarray(w, np.float32).astype(ml_dtypes.bfloat16)).reshape(k // 32, 32, n)
    amax = np.abs(w).max(1)
    mant, ex = np.frexp(amax / 6.0)
    byte = np.clip(np.where(amax > 0, np.where(mant > 0.5, ex, ex - 1) + 127, 1), 1, 254)
    scaled = (w * np.exp2(127.0 - byte)[:, None, :]).reshape(k, n).astype(np.float32)
    c = np.ascontiguousarray(scaled.reshape(k // 512, 128, 4, n).transpose(0, 1, 3, 2)).astype(ml_dtypes.float4_e2m1fn).view(np.uint8) & 0xF
    words = (c[..., 0::2] | (c[..., 1::2] << 4)).reshape(k // 512, 128, 2 * n)
    return np.ascontiguousarray(words), np.ascontiguousarray(byte.astype(np.uint8).reshape(k // 512, 16, n))


def unpack_fp4(words, scales):
    g, _, n = scales.shape
    words = np.ascontiguousarray(words).reshape(g, 128, n, 2)
    nib = np.empty((g, 128, n, 4), np.uint8)
    nib[..., 0::2] = words & 0xF
    nib[..., 1::2] = words >> 4
    vals = E2M1[nib] * np.repeat(np.exp2(scales.astype(np.float64) - 127.0), 8, axis=1)[..., None]
    return vals.transpose(0, 1, 3, 2).reshape(g * 512, n)


def relu(v):
    return np.maximum(v, 0.0)


K, T, S, D, N, H = 1024, 2048, 512, 4, 128, 512


def setup_inputs():
    n = np.random.standard_normal
    s = mx_kscale(K)[:, None]
    u = mx_kscale(H)
    packed_xT = pack_weight(n((K, T)) * s)
    packed_w1 = pack_fp4(n((K, H)) / np.sqrt(K) / s)
    packed_w2 = pack_fp4(n((K, H)) / np.sqrt(K) / s)
    packed_w3 = pack_fp4(n((H, N)) / np.sqrt(H) / u[:, None])
    return {
        "x_words": packed_xT[0],
        "x_scales": packed_xT[1],
        "w1_words": packed_w1[0],
        "w1_scales": packed_w1[1],
        "w2_words": packed_w2[0],
        "w2_scales": packed_w2[1],
        "slo": (np.random.uniform(0.5, 2.0, (H, S))).astype(np.float32),
        "unit": (np.random.uniform(0.6, 1.4, (H, 1)) * u[:, None]).astype(np.float32),
        "w3_words": packed_w3[0],
        "w3_scales": packed_w3[1],
        "offs": striped(np.random.permutation(T)[:S]),
        "pl": striped(np.random.permutation(S)),
    }


def reference(x_words, x_scales, w1_words, w1_scales, w2_words, w2_scales, slo, unit, w3_words, w3_scales, offs, pl):
    xq = unpack_weight(x_words, x_scales)[:, unstriped(offs)]
    pf = unpack_fp4(w1_words, w1_scales).T @ xq
    pref = np.log(np.exp(pf) + 1.0)
    queue = pref.reshape(len(pref), -1, D).sum(axis=2)
    wait = np.repeat(queue, D, axis=1) - pref
    dc = unpack_fp4(w2_words, w2_scales).T @ xq
    deco = np.log(np.exp(dc) + 1.0)
    dp = deco[:, unstriped(pl)]
    intf = wait / (deco + dp + 0.5)
    slack = f64(slo) - intf
    ip = intf[:, unstriped(pl)]
    hid = f64(unit) * (relu(slack) - (0.5 * ip))
    return unpack_fp4(w3_words, w3_scales).T @ mxq(hid, 0, "e4m3")

@@ -1,0 +1,234 @@
+from contextlib import ExitStack
+
+import concourse.mybir as mybir
+from concourse.masks import make_identity
+
+K, T, S, D, N, H = 1024, 2048, 512, 4, 128, 512
+FLOPS = 2 * K * H * S * 2 + 2 * H * N * S
+
+F32 = mybir.dt.float32
+BF16 = mybir.dt.bfloat16
+I32 = mybir.dt.int32
+U32 = mybir.dt.uint32
+U16 = mybir.dt.uint16
+U8 = mybir.dt.uint8
+FP8X4 = mybir.dt.float8_e4m3fn_x4
+FP4X4 = mybir.dt.float4_e2m1fn_x4
+ACT = mybir.ActivationFunctionType
+ALU = mybir.AluOpType
+
+P = 128
+PACK = 4
+PASSES = K // (P * PACK)
+GROUPS = S // D
+HALF = S // 2
+LIST_COLS = HALF // 16
+CLAMP = 32.0
+FLOOR = 1.0e-18
+HUGE = 3.0e38
+
+
+def tile_picked_ypdsch_late_p_kernel(tc, x_words, x_scales, w1_words, w1_scales, w2_words, w2_scales, slo, unit, w3_words, w3_scales, offs, pl, out):
+    nc = tc.nc
+    with ExitStack() as ctx:
+        lists = ctx.enter_context(tc.tile_pool(name="lists", bufs=1))
+        keep = ctx.enter_context(tc.tile_pool(name="keep", bufs=1))
+        psum = ctx.enter_context(tc.psum_pool(name="psum", bufs=1))
+
+        offs_sb = lists.tile([P, S // 16], U16)
+        pl_sb = lists.tile([P, S // 16], U16)
+
+        xs = keep.tile([P, PASSES, T], U8, align_bytes=64)
+        wsc = keep.tile([P, 2 * PASSES * H + N], U8, align_bytes=64)
+        nc.vector.memset(xs[:].rearrange("p o n -> p (o n)").bitcast(I32), 0)
+        nc.vector.memset(wsc[:].bitcast(I32), 0)
+        w1s = wsc[:, 0 : PASSES * H]
+        w2s = wsc[:, PASSES * H : 2 * PASSES * H]
+        w3s = wsc[:, 2 * PASSES * H :]
+
+        xw = [keep.tile([P, T], U32, name=f"xw{o}", tag=f"xw{o}") for o in range(PASSES)]
+        w1w = keep.tile([P, PASSES, 2 * H], U8, align_bytes=64)
+        w2w = keep.tile([P, PASSES, 2 * H], U8, align_bytes=64)
+        w3w = keep.tile([P, 2 * N], U8, align_bytes=64)
+        unit_sb = keep.tile([P, PACK], F32)
+
+        def load_scales(dst, src):
+            passes = src.shape[0]
+            for q in range(4):
+                nc.scalar.dma_start(
+                    dst[32 * q : 32 * q + 4, :].bitcast(I32).rearrange("r (o n) -> r o n", o=passes),
+                    src[:, 4 * q : 4 * q + 4, :].rearrange("o r n -> r o n").bitcast(I32),
+                )
+
+        nc.sync.dma_start(offs_sb[:], offs)
+        nc.sync.dma_start(xw[0][:].bitcast(I32), x_words[0].rearrange("p n t -> p (n t)").bitcast(I32))
+        load_scales(xs[:].rearrange("p o n -> p (o n)"), x_scales)
+        nc.sync.dma_start(w2w[:].bitcast(I32), w2_words.rearrange("o p n -> p o n").bitcast(I32))
+        nc.sync.dma_start(xw[1][:].bitcast(I32), x_words[1].rearrange("p n t -> p (n t)").bitcast(I32))
+        load_scales(w2s, w2_scales)
+        nc.sync.dma_start(w1w[:].bitcast(I32), w1_words.rearrange("o p n -> p o n").bitcast(I32))
+        load_scales(w1s, w1_scales)
+        nc.sync.dma_start(pl_sb[:], pl)
+        nc.sync.dma_start(unit_sb[:], unit.rearrange("(p t) o -> p (t o)", t=PACK))
+
+        ident = keep.tile([P, P], F32)
+        make_identity(nc, ident[:])
+
+        xb = keep.tile([P, PASSES, S], U8, align_bytes=64)
+        xbd = keep.tile([P, PASSES, S], U8, align_bytes=64)
+        xg = [keep.tile([P, S], U32, name=f"xg{o}", align_bytes=64) for o in range(PASSES)]
+        w2d = keep.tile([P, PASSES, 2 * H], U8, align_bytes=64)
+        w2sd = keep.tile([P, PASSES * H], U8, align_bytes=64)
+        for o in range(PASSES):
+            nc.vector.tensor_copy(xb[:, o, :], xs[:, o, :].indirect(offs_sb[:]))
+        nc.vector.tensor_copy(xg[0][:], xw[0][:].indirect(offs_sb[:]))
+        nc.vector.tensor_copy(
+            w2d[:].bitcast(U16).rearrange("p o (t m) -> p o t m", t=PACK),
+            w2w[:].bitcast(U16).rearrange("p o (m t) -> p o t m", t=PACK),
+        )
+        nc.vector.tensor_copy(
+            w2sd[:].rearrange("p (o t m) -> p o t m", o=PASSES, t=PACK),
+            w2s.rearrange("p (o m t) -> p o t m", o=PASSES, t=PACK),
+        )
+        nc.vector.tensor_copy(xg[1][:], xw[1][:].indirect(offs_sb[:]))
+        slo_sb = keep.tile([P, PACK, S], F32, tag="xw0")
+        nc.sync.dma_start(slo_sb[:], slo.rearrange("(p t) s -> p t s", t=PACK))
+        nc.sync.dma_start(w3w[:].bitcast(I32), w3_words[0].bitcast(I32))
+        load_scales(w3s, w3_scales)
+        xgd = keep.tile([P, PASSES, S], U32, align_bytes=64)
+        nc.vector.tensor_copy(
+            xbd[:].rearrange("p o (d v) -> p o d v", d=D), xb[:].rearrange("p o (v d) -> p o d v", d=D)
+        )
+        for o in range(PASSES):
+            nc.vector.tensor_copy(xgd[:, o, :].rearrange("p (d v) -> p d v", d=D), xg[o][:].rearrange("p (v d) -> p d v", d=D))
+
+        half_unit = keep.tile([P, PACK], F32)
+        upper = keep.tile([P, PACK], F32)
+        lower = keep.tile([P, PACK], F32)
+        nc.vector.tensor_scalar(half_unit[:], unit_sb[:], 2.0, None, ALU.mult)
+        nc.vector.tensor_scalar(upper[:], unit_sb[:], 0.0, HUGE, ALU.is_ge, ALU.mult)
+        nc.vector.tensor_scalar(lower[:], unit_sb[:], 0.0, -HUGE, ALU.is_lt, ALU.mult)
+
+        dc = [psum.tile([P, S], F32, name=f"dc{t}") for t in range(PACK)]
+        pf = [psum.tile([P, H], F32, name=f"pf{d}") for d in range(D)]
+        for o in range(PASSES):
+            for t in range(PACK):
+                nc.tensor.matmul_mx(
+                    out=dc[t][:],
+                    lhsT=w2d[:, o, 2 * P * t : 2 * P * (t + 1)].bitcast(FP4X4),
+                    lhsT_scale=w2sd[:, o * H + P * t : o * H + P * (t + 1)],
+                    rhs=xg[o][:].bitcast(FP8X4),
+                    rhs_scale=xb[:, o, :],
+                    start=(o == 0),
+                    stop=(o == PASSES - 1),
+                )
+        for o in range(PASSES):
+            for d in range(D):
+                nc.tensor.matmul_mx(
+                    out=pf[d][:],
+                    lhsT=xgd[:, o, P * d : P * (d + 1)].bitcast(FP8X4),
+                    lhsT_scale=xbd[:, o, P * d : P * (d + 1)],
+                    rhs=w1w[:, o, :].bitcast(FP4X4),
+                    rhs_scale=w1s[:, o * H : (o + 1) * H],
+                    start=(o == 0),
+                    stop=(o == PASSES - 1),
+                )
+
+        def in_list_order(bank):
+            return bank[:].rearrange("p (d v) -> p v d", d=D)
+
+        def by_group(rows):
+            return rows.rearrange("p (v d) -> p v d", d=D)
+
+        def dealt(bank):
+            return bank[:].rearrange("p (m t) -> p t m", t=PACK)
+
+        clamped = keep.tile([P, D, PACK, P], F32, tag="clamped_then_logs")
+        excess = keep.tile([P, D, PACK, P], F32)
+        sig_dc = keep.tile([P, PACK, S], F32)
+        sig_pf = keep.tile([P, D, PACK, P], F32)
+        for t in range(PACK):
+            nc.scalar.activation(sig_dc[:, t, :], dc[t][:], ACT.Sigmoid, scale=-1.0)
+        for d in range(D):
+            nc.vector.tensor_scalar(clamped[:, d], dealt(pf[d]), CLAMP, None, ALU.min)
+        for d in range(D):
+            nc.scalar.activation(sig_pf[:, d], clamped[:, d], ACT.Sigmoid, scale=-1.0)
+        for d in range(D):
+            nc.vector.tensor_tensor(excess[:, d], clamped[:, d], dealt(pf[d]), ALU.subtract)
+
+        scaled_slo = keep.tile([P, PACK, S], F32)
+        for t in range(PACK):
+            nc.gpsimd.tensor_scalar(scaled_slo[:, t, :], slo_sb[:, t, :], unit_sb[:, t : t + 1], 0.0, ALU.mult, ALU.add)
+
+        logs = keep.tile([P, 2, PACK, S], F32, tag="clamped_then_logs")
+        for t in range(PACK):
+            nc.scalar.activation(logs[:, 0, t, :], sig_dc[:, t, :], ACT.Ln, bias=FLOOR)
+        for t in range(PACK):
+            nc.scalar.activation(logs[:, 1, t, :].rearrange("p (d m) -> p d m", d=D), sig_pf[:, :, t, :], ACT.Ln)
+
+        waits = [psum.tile([P, S], F32, name=f"wait{t}", tag=f"pf{t}") for t in range(PACK)]
+        others = [(d, e) for d in range(D) for e in range(D) if e != d]
+        for t in range(PACK):
+            for i, (d, e) in enumerate(others):
+                nc.tensor.matmul(waits[t][:, P * d : P * (d + 1)], excess[:, e, t, :], ident[:], start=(i == 0), stop=False, is_transpose=True)
+        for t in range(PACK):
+            for i, (d, e) in enumerate(others):
+                nc.tensor.matmul(waits[t][:, P * d : P * (d + 1)], logs[:, 1, t, P * e : P * (e + 1)], ident[:], start=False, stop=(i == len(others) - 1), is_transpose=True)
+
+        halves = [(slice(h * HALF, (h + 1) * HALF), pl_sb[:, h * LIST_COLS : (h + 1) * LIST_COLS]) for h in range(2)]
+        deco = [keep.tile([P, S], F32, name=f"deco{t}") for t in range(PACK)]
+        deco_plus = keep.tile([P, PACK, S], F32)
+        den = keep.tile([P, PACK, S], F32, tag="den_then_rec")
+        for t in range(PACK):
+            nc.vector.scalar_tensor_tensor(deco[t][:], logs[:, 0, t, :], -1.0, dc[t][:], ALU.mult, ALU.max)
+            nc.gpsimd.tensor_scalar(deco_plus[:, t, :], deco[t][:], 1.0, 0.5, ALU.mult, ALU.add)
+        for t in range(PACK):
+            for cols, part in halves:
+                nc.vector.tensor_tensor(den[:, t, cols], deco[t][:].indirect(part), deco_plus[:, t, cols], ALU.add)
+
+        root = keep.tile([P, PACK, S], F32)
+        for t in range(PACK):
+            nc.scalar.activation(root[:, t, :], den[:, t, :], ACT.Ln, scale=4.0, bias=-1.0)
+        rec = keep.tile([P, PACK, S], F32, tag="den_then_rec")
+        for t in range(PACK):
+            nc.scalar.activation(rec[:, t, :], root[:, t, :], ACT.Sigmoid, scale=-1.0)
+
+        push = [keep.tile([P, S], F32, name=f"push{t}") for t in range(PACK)]
+        room = keep.tile([P, PACK, S], F32)
+        kept = keep.tile([P, PACK, S], F32)
+        hid = keep.tile([P, 2, PACK, HALF], F32)
+
+        def gather_hid(t, h):
+            cols, part = halves[h]
+            nc.vector.tensor_tensor(hid[:, h, t, :], push[t][:].indirect(part), kept[:, t, cols], ALU.add)
+
+        for t in range(PACK):
+            nc.vector.scalar_tensor_tensor(by_group(push[t][:]), in_list_order(waits[t]), half_unit[:, t : t + 1], by_group(rec[:, t, :]), ALU.mult, ALU.mult)
+            if t > 0:
+                nc.vector.tensor_scalar(kept[:, t - 1, :], room[:, t - 1, :], upper[:, t - 1 : t], lower[:, t - 1 : t], ALU.min, ALU.max)
+            nc.vector.scalar_tensor_tensor(room[:, t, :], push[t][:], 2.0, scaled_slo[:, t, :], ALU.mult, ALU.add)
+            if t > 0:
+                gather_hid(t - 1, 0)
+        last = PACK - 1
+        gather_hid(0, 1)
+        nc.vector.tensor_scalar(kept[:, last, :], room[:, last, :], upper[:, last:], lower[:, last:], ALU.min, ALU.max)
+        gather_hid(1, 1)
+        gather_hid(last, 0)
+        gather_hid(2, 1)
+        gather_hid(last, 1)
+
+        for h in range(2):
+            hb = keep.tile([P, HALF, PACK], BF16, name=f"hb{h}", align_bytes=64)
+            codes = keep.tile([P, HALF], U32, name=f"codes{h}", align_bytes=64)
+            hs = keep.tile([P, HALF], U8, name=f"hs{h}", align_bytes=64)
+            src = hid[:, h].rearrange("p t c -> p c t")
+            if h == 0:
+                nc.scalar.copy(hb[:], src)
+            else:
+                nc.vector.tensor_copy(hb[:], src)
+            nc.vector.quantize_mx(out=codes[:].bitcast(FP8X4), scales=hs[:], in_=hb[:].rearrange("p c t -> p (c t)"))
+            acc = psum.tile([P, HALF], F32, name=f"acc{h}", tag=f"dc{h}")
+            nc.tensor.matmul_mx(out=acc[:], lhsT=w3w[:].bitcast(FP4X4), lhsT_scale=w3s, rhs=codes[:].bitcast(FP8X4), rhs_scale=hs[:], start=True, stop=True)
+            res = keep.tile([P, HALF], F32, name=f"res{h}")
+            nc.scalar.copy(res[:], acc[:])
+            nc.sync.dma_start(out[:, halves[h][0]], res[:])

@@ -38,74 +38,79 @@ def tile_picked_ypdsch_late_p_kernel(tc, x_words, x_scales, w1_words, w1_scales,
         offs_sb = lists.tile([P, S // 16], U16)
         pl_sb = lists.tile([P, S // 16], U16)
 
-        xs = keep.tile([P, PASSES, T], U8, align_bytes=64)
-        wsc = keep.tile([P, 2 * PASSES * H + N], U8, align_bytes=64)
-        nc.vector.memset(xs[:].rearrange("p o n -> p (o n)").bitcast(I32), 0)
-        nc.vector.memset(wsc[:].bitcast(I32), 0)
-        w1s = wsc[:, 0 : PASSES * H]
-        w2s = wsc[:, PASSES * H : 2 * PASSES * H]
-        w3s = wsc[:, 2 * PASSES * H :]
+        xs = keep.tile([P, PASSES, T], U8, align_bytes=64, tag="xs")
+        w2s = keep.tile([P, PASSES, H], U8, align_bytes=64, tag="w2s")
+        w1s = keep.tile([P, PASSES, H], U8, align_bytes=64)
+        for plane in (xs, w2s, w1s):
+            nc.vector.memset(plane[:].bitcast(I32), 0)
 
-        xw = [keep.tile([P, T], U32, name=f"xw{o}", tag=f"xw{o}") for o in range(PASSES)]
+        xw = [keep.tile([P, T], U32, name=f"xw{o}", tag=f"xw{o}", align_bytes=64) for o in range(PASSES)]
         w1w = keep.tile([P, PASSES, 2 * H], U8, align_bytes=64)
-        w2w = keep.tile([P, PASSES, 2 * H], U8, align_bytes=64)
-        w3w = keep.tile([P, 2 * N], U8, align_bytes=64)
+        w2w = keep.tile([P, PASSES, 2 * H], U8, align_bytes=64, tag="w2w")
         unit_sb = keep.tile([P, PACK], F32)
 
-        def load_scales(dst, src):
-            passes = src.shape[0]
+        def load_scales(queue, dst, src):
             for q in range(4):
-                nc.scalar.dma_start(
-                    dst[32 * q : 32 * q + 4, :].bitcast(I32).rearrange("r (o n) -> r o n", o=passes),
+                queue.dma_start(
+                    dst[32 * q : 32 * q + 4].bitcast(I32),
                     src[:, 4 * q : 4 * q + 4, :].rearrange("o r n -> r o n").bitcast(I32),
                 )
 
+        def load_x_words(o):
+            nc.sync.dma_start(xw[o][:].bitcast(I32), x_words[o].rearrange("p n t -> p (n t)").bitcast(I32))
+
+        def load_w_words(dst, src):
+            nc.sync.dma_start(dst[:].bitcast(I32), src.rearrange("o p n -> p o n").bitcast(I32))
+
         nc.sync.dma_start(offs_sb[:], offs)
-        nc.sync.dma_start(xw[0][:].bitcast(I32), x_words[0].rearrange("p n t -> p (n t)").bitcast(I32))
-        load_scales(xs[:].rearrange("p o n -> p (o n)"), x_scales)
-        nc.sync.dma_start(w2w[:].bitcast(I32), w2_words.rearrange("o p n -> p o n").bitcast(I32))
-        nc.sync.dma_start(xw[1][:].bitcast(I32), x_words[1].rearrange("p n t -> p (n t)").bitcast(I32))
-        load_scales(w2s, w2_scales)
-        nc.sync.dma_start(w1w[:].bitcast(I32), w1_words.rearrange("o p n -> p o n").bitcast(I32))
-        load_scales(w1s, w1_scales)
+        load_w_words(w2w, w2_words)
+        load_x_words(0)
+        load_scales(nc.scalar, xs, x_scales)
+        load_scales(nc.sync, w2s, w2_scales)
+        load_x_words(1)
         nc.sync.dma_start(pl_sb[:], pl)
-        nc.sync.dma_start(unit_sb[:], unit.rearrange("(p t) o -> p (t o)", t=PACK))
+        load_w_words(w1w, w1_words)
+        load_scales(nc.scalar, w1s, w1_scales)
+        nc.gpsimd.dma_start(unit_sb[:], unit.rearrange("(p t) o -> p (t o)", t=PACK))
 
         ident = keep.tile([P, P], F32)
         make_identity(nc, ident[:])
 
-        xb = keep.tile([P, PASSES, S], U8, align_bytes=64)
-        xbd = keep.tile([P, PASSES, S], U8, align_bytes=64)
-        xg = [keep.tile([P, S], U32, name=f"xg{o}", align_bytes=64) for o in range(PASSES)]
-        w2d = keep.tile([P, PASSES, 2 * H], U8, align_bytes=64)
-        w2sd = keep.tile([P, PASSES * H], U8, align_bytes=64)
-        for o in range(PASSES):
-            nc.vector.tensor_copy(xb[:, o, :], xs[:, o, :].indirect(offs_sb[:]))
-        nc.vector.tensor_copy(xg[0][:], xw[0][:].indirect(offs_sb[:]))
-        nc.vector.tensor_copy(
-            w2d[:].bitcast(U16).rearrange("p o (t m) -> p o t m", t=PACK),
-            w2w[:].bitcast(U16).rearrange("p o (m t) -> p o t m", t=PACK),
-        )
-        nc.vector.tensor_copy(
-            w2sd[:].rearrange("p (o t m) -> p o t m", o=PASSES, t=PACK),
-            w2s.rearrange("p (o m t) -> p o t m", o=PASSES, t=PACK),
-        )
-        nc.vector.tensor_copy(xg[1][:], xw[1][:].indirect(offs_sb[:]))
-        slo_sb = keep.tile([P, PACK, S], F32, tag="xw0")
-        nc.sync.dma_start(slo_sb[:], slo.rearrange("(p t) s -> p t s", t=PACK))
-        nc.sync.dma_start(w3w[:].bitcast(I32), w3_words[0].bitcast(I32))
-        load_scales(w3s, w3_scales)
+        xg = keep.tile([P, PASSES, S], U32, align_bytes=64)
         xgd = keep.tile([P, PASSES, S], U32, align_bytes=64)
-        nc.vector.tensor_copy(
-            xbd[:].rearrange("p o (d v) -> p o d v", d=D), xb[:].rearrange("p o (v d) -> p o d v", d=D)
-        )
-        for o in range(PASSES):
-            nc.vector.tensor_copy(xgd[:, o, :].rearrange("p (d v) -> p d v", d=D), xg[o][:].rearrange("p (v d) -> p d v", d=D))
+        w2d = keep.tile([P, PASSES, 2 * H], U8, align_bytes=64)
+        w2sd = keep.tile([P, PASSES, H], U8, align_bytes=64)
 
-        half_unit = keep.tile([P, PACK], F32)
+        def deal(dst, src, run):
+            nc.vector.tensor_copy(
+                dst.rearrange("p o (t c i) -> p o c t i", t=PACK, i=run),
+                src.rearrange("p o (c i t) -> p o c t i", t=PACK, i=run),
+            )
+
+        deal(w2d[:].bitcast(U16), w2w[:].bitcast(U16), 8)
+        w3w = keep.tile([P, 1, 2 * N], U8, align_bytes=64, tag="w2w")
+        xb0 = keep.tile([P, S], U8, align_bytes=64, tag="xb0")
+        nc.vector.tensor_copy(xb0[:], xs[:, 0, :].indirect(offs_sb[:]))
+        nc.vector.tensor_copy(xg[:, 0, :], xw[0][:].indirect(offs_sb[:]))
+        deal(w2sd[:], w2s[:], 16)
+        xb1 = keep.tile([P, S], U8, align_bytes=64, tag="w2s")
+        nc.vector.tensor_copy(xb1[:], xs[:, 1, :].indirect(offs_sb[:]))
+        xb = [xb0, xb1]
+        nc.vector.tensor_copy(xg[:, 1, :], xw[1][:].indirect(offs_sb[:]))
+        xbd = keep.tile([P, PASSES, S], U8, align_bytes=64, tag="xw1")
+        for o in range(PASSES):
+            deal(xbd[:, o : o + 1, :], xb[o][:].unsqueeze(1), 16)
+        deal(xgd[:], xg[:], 4)
+        slo_sb = keep.tile([P, PACK, S], F32, align_bytes=64, tag="xs")
+        nc.sync.dma_start(slo_sb[:], slo.rearrange("(p t) s -> p t s", t=PACK))
+        load_w_words(w3w, w3_words)
+
+        twice_unit = keep.tile([P, PACK], F32)
+        half_unit = keep.tile([P, 1], F32)
         upper = keep.tile([P, PACK], F32)
         lower = keep.tile([P, PACK], F32)
-        nc.vector.tensor_scalar(half_unit[:], unit_sb[:], 2.0, None, ALU.mult)
+        nc.vector.tensor_scalar(twice_unit[:], unit_sb[:], 2.0, None, ALU.mult)
+        nc.vector.tensor_scalar(half_unit[:], unit_sb[:, PACK - 1 :], 0.5, None, ALU.mult)
         nc.vector.tensor_scalar(upper[:], unit_sb[:], 0.0, HUGE, ALU.is_ge, ALU.mult)
         nc.vector.tensor_scalar(lower[:], unit_sb[:], 0.0, -HUGE, ALU.is_lt, ALU.mult)
 
@@ -116,23 +121,27 @@ def tile_picked_ypdsch_late_p_kernel(tc, x_words, x_scales, w1_words, w1_scales,
                 nc.tensor.matmul_mx(
                     out=dc[t][:],
                     lhsT=w2d[:, o, 2 * P * t : 2 * P * (t + 1)].bitcast(FP4X4),
-                    lhsT_scale=w2sd[:, o * H + P * t : o * H + P * (t + 1)],
-                    rhs=xg[o][:].bitcast(FP8X4),
-                    rhs_scale=xb[:, o, :],
+                    lhsT_scale=w2sd[:, o, P * t : P * (t + 1)],
+                    rhs=xg[:, o, :].bitcast(FP8X4),
+                    rhs_scale=xb[o][:],
                     start=(o == 0),
                     stop=(o == PASSES - 1),
                 )
-        for o in range(PASSES):
-            for d in range(D):
+        for d in range(D):
+            for o in range(PASSES):
                 nc.tensor.matmul_mx(
                     out=pf[d][:],
                     lhsT=xgd[:, o, P * d : P * (d + 1)].bitcast(FP8X4),
                     lhsT_scale=xbd[:, o, P * d : P * (d + 1)],
                     rhs=w1w[:, o, :].bitcast(FP4X4),
-                    rhs_scale=w1s[:, o * H : (o + 1) * H],
+                    rhs_scale=w1s[:, o, :],
                     start=(o == 0),
                     stop=(o == PASSES - 1),
                 )
+
+        w3s = keep.tile([P, 1, N], U8, align_bytes=64, tag="xb0")
+        nc.vector.memset(w3s[:].bitcast(I32), 0)
+        load_scales(nc.sync, w3s, w3_scales)
 
         def in_list_order(bank):
             return bank[:].rearrange("p (d v) -> p v d", d=D)
@@ -158,7 +167,7 @@ def tile_picked_ypdsch_late_p_kernel(tc, x_words, x_scales, w1_words, w1_scales,
 
         scaled_slo = keep.tile([P, PACK, S], F32)
         for t in range(PACK):
-            nc.gpsimd.tensor_scalar(scaled_slo[:, t, :], slo_sb[:, t, :], unit_sb[:, t : t + 1], 0.0, ALU.mult, ALU.add)
+            nc.vector.tensor_scalar(scaled_slo[:, t, :], slo_sb[:, t, :], unit_sb[:, t : t + 1], None, ALU.mult)
 
         logs = keep.tile([P, 2, PACK, S], F32, tag="clamped_then_logs")
         for t in range(PACK):
@@ -167,7 +176,7 @@ def tile_picked_ypdsch_late_p_kernel(tc, x_words, x_scales, w1_words, w1_scales,
             nc.scalar.activation(logs[:, 1, t, :].rearrange("p (d m) -> p d m", d=D), sig_pf[:, :, t, :], ACT.Ln)
 
         waits = [psum.tile([P, S], F32, name=f"wait{t}", tag=f"pf{t}") for t in range(PACK)]
-        others = [(d, e) for d in range(D) for e in range(D) if e != d]
+        others = [(d, e) for e in range(D) for d in range(D) if e != d]
         for t in range(PACK):
             for i, (d, e) in enumerate(others):
                 nc.tensor.matmul(waits[t][:, P * d : P * (d + 1)], excess[:, e, t, :], ident[:], start=(i == 0), stop=False, is_transpose=True)
@@ -181,54 +190,61 @@ def tile_picked_ypdsch_late_p_kernel(tc, x_words, x_scales, w1_words, w1_scales,
         den = keep.tile([P, PACK, S], F32, tag="den_then_rec")
         for t in range(PACK):
             nc.vector.scalar_tensor_tensor(deco[t][:], logs[:, 0, t, :], -1.0, dc[t][:], ALU.mult, ALU.max)
-            nc.gpsimd.tensor_scalar(deco_plus[:, t, :], deco[t][:], 1.0, 0.5, ALU.mult, ALU.add)
+            engine = nc.gpsimd if t < PACK - 1 else nc.vector
+            engine.tensor_scalar(deco_plus[:, t, :], deco[t][:], 1.0, 0.5, ALU.mult, ALU.add)
+        last = PACK - 1
+        den_tail = keep.tile([P, HALF], F32)
+        rec_tail = keep.tile([P, HALF], F32)
         for t in range(PACK):
-            for cols, part in halves:
-                nc.vector.tensor_tensor(den[:, t, cols], deco[t][:].indirect(part), deco_plus[:, t, cols], ALU.add)
+            for h, (cols, part) in enumerate(halves):
+                dst = den_tail[:] if (t, h) == (last, 1) else den[:, t, cols]
+                nc.vector.tensor_tensor(dst, deco[t][:].indirect(part), deco_plus[:, t, cols], ALU.add)
+        nc.vector.reciprocal(rec_tail[:], den_tail[:])
 
+        by_tables = [slice(0, S)] * last + [halves[0][0]]
         root = keep.tile([P, PACK, S], F32)
-        for t in range(PACK):
-            nc.scalar.activation(root[:, t, :], den[:, t, :], ACT.Ln, scale=4.0, bias=-1.0)
+        for t, cols in enumerate(by_tables):
+            nc.scalar.activation(root[:, t, cols], den[:, t, cols], ACT.Ln, scale=4.0, bias=-1.0)
         rec = keep.tile([P, PACK, S], F32, tag="den_then_rec")
-        for t in range(PACK):
-            nc.scalar.activation(rec[:, t, :], root[:, t, :], ACT.Sigmoid, scale=-1.0)
+        for t, cols in enumerate(by_tables):
+            nc.scalar.activation(rec[:, t, cols], root[:, t, cols], ACT.Sigmoid, scale=-1.0)
 
         push = [keep.tile([P, S], F32, name=f"push{t}") for t in range(PACK)]
         room = keep.tile([P, PACK, S], F32)
         kept = keep.tile([P, PACK, S], F32)
-        hid = keep.tile([P, 2, PACK, HALF], F32)
+        picked = keep.tile([P, 2, PACK, HALF], F32)
 
-        def gather_hid(t, h):
-            cols, part = halves[h]
-            nc.vector.tensor_tensor(hid[:, h, t, :], push[t][:].indirect(part), kept[:, t, cols], ALU.add)
-
-        for t in range(PACK):
-            nc.vector.scalar_tensor_tensor(by_group(push[t][:]), in_list_order(waits[t]), half_unit[:, t : t + 1], by_group(rec[:, t, :]), ALU.mult, ALU.mult)
-            if t > 0:
-                nc.vector.tensor_scalar(kept[:, t - 1, :], room[:, t - 1, :], upper[:, t - 1 : t], lower[:, t - 1 : t], ALU.min, ALU.max)
-            nc.vector.scalar_tensor_tensor(room[:, t, :], push[t][:], 2.0, scaled_slo[:, t, :], ALU.mult, ALU.add)
-            if t > 0:
-                gather_hid(t - 1, 0)
-        last = PACK - 1
-        gather_hid(0, 1)
-        nc.vector.tensor_scalar(kept[:, last, :], room[:, last, :], upper[:, last:], lower[:, last:], ALU.min, ALU.max)
-        gather_hid(1, 1)
-        gather_hid(last, 0)
-        gather_hid(2, 1)
-        gather_hid(last, 1)
+        for step in range(PACK + 2):
+            t = step
+            if t < PACK:
+                cols = by_tables[t]
+                groups = slice(cols.start // D, cols.stop // D)
+                nc.vector.scalar_tensor_tensor(by_group(push[t][:, cols]), in_list_order(waits[t])[:, groups, :], twice_unit[:, t : t + 1], by_group(rec[:, t, cols]), ALU.mult, ALU.mult)
+            if t == last:
+                nc.vector.scalar_tensor_tensor(by_group(push[t][:, HALF:]), in_list_order(waits[t])[:, HALF // D :, :], half_unit[:], by_group(rec_tail[:]), ALU.mult, ALU.mult)
+            t = step - 1
+            if 0 <= t < PACK:
+                nc.vector.scalar_tensor_tensor(room[:, t, :], push[t][:], 2.0, scaled_slo[:, t, :], ALU.mult, ALU.add)
+            t = step - 2
+            if 0 <= t < PACK:
+                nc.vector.tensor_scalar(kept[:, t, :], room[:, t, :], upper[:, t : t + 1], lower[:, t : t + 1], ALU.min, ALU.max)
+        for h in range(2):
+            for t in range(PACK):
+                nc.scalar.activation(picked[:, h, t, :], push[t][:].indirect(halves[h][1]), ACT.Copy)
 
         for h in range(2):
             hb = keep.tile([P, HALF, PACK], BF16, name=f"hb{h}", align_bytes=64)
             codes = keep.tile([P, HALF], U32, name=f"codes{h}", align_bytes=64)
             hs = keep.tile([P, HALF], U8, name=f"hs{h}", align_bytes=64)
-            src = hid[:, h].rearrange("p t c -> p c t")
-            if h == 0:
-                nc.scalar.copy(hb[:], src)
-            else:
-                nc.vector.tensor_copy(hb[:], src)
+            nc.vector.tensor_tensor(
+                hb[:].rearrange("p (c i) t -> p c t i", i=4),
+                picked[:, h].rearrange("p t (c i) -> p c t i", i=4),
+                kept[:, :, halves[h][0]].rearrange("p t (c i) -> p c t i", i=4),
+                ALU.add,
+            )
             nc.vector.quantize_mx(out=codes[:].bitcast(FP8X4), scales=hs[:], in_=hb[:].rearrange("p c t -> p (c t)"))
             acc = psum.tile([P, HALF], F32, name=f"acc{h}", tag=f"dc{h}")
-            nc.tensor.matmul_mx(out=acc[:], lhsT=w3w[:].bitcast(FP4X4), lhsT_scale=w3s, rhs=codes[:].bitcast(FP8X4), rhs_scale=hs[:], start=True, stop=True)
+            nc.tensor.matmul_mx(out=acc[:], lhsT=w3w[:, 0, :].bitcast(FP4X4), lhsT_scale=w3s[:, 0, :], rhs=codes[:].bitcast(FP8X4), rhs_scale=hs[:], start=True, stop=True)
             res = keep.tile([P, HALF], F32, name=f"res{h}")
             nc.scalar.copy(res[:], acc[:])
             nc.sync.dma_start(out[:, halves[h][0]], res[:])

@@ -49,8 +49,8 @@ def tile_picked_ypdsch_late_p_kernel(tc, x_words, x_scales, w1_words, w1_scales,
         w2w = keep.tile([P, PASSES, 2 * H], U8, align_bytes=64, tag="w2w")
         unit_sb = keep.tile([P, PACK], F32)
 
-        def load_scales(queue, dst, src):
-            for q in range(4):
+        def load_scales(queue, dst, src, quadrants=range(4)):
+            for q in quadrants:
                 queue.dma_start(
                     dst[32 * q : 32 * q + 4].bitcast(I32),
                     src[:, 4 * q : 4 * q + 4, :].rearrange("o r n -> r o n").bitcast(I32),
@@ -63,10 +63,12 @@ def tile_picked_ypdsch_late_p_kernel(tc, x_words, x_scales, w1_words, w1_scales,
             nc.sync.dma_start(dst[:].bitcast(I32), src.rearrange("o p n -> p o n").bitcast(I32))
 
         nc.sync.dma_start(offs_sb[:], offs)
+        load_scales(nc.sync, xs, x_scales, range(0, 1))
+        load_scales(nc.scalar, xs, x_scales, range(1, 4))
         load_w_words(w2w, w2_words)
         load_x_words(0)
-        load_scales(nc.scalar, xs, x_scales)
-        load_scales(nc.sync, w2s, w2_scales)
+        load_scales(nc.sync, w2s, w2_scales, range(0, 2))
+        load_scales(nc.scalar, w2s, w2_scales, range(2, 4))
         load_x_words(1)
         nc.sync.dma_start(pl_sb[:], pl)
         load_w_words(w1w, w1_words)
@@ -79,7 +81,6 @@ def tile_picked_ypdsch_late_p_kernel(tc, x_words, x_scales, w1_words, w1_scales,
         xg = keep.tile([P, PASSES, S], U32, align_bytes=64)
         xgd = keep.tile([P, PASSES, S], U32, align_bytes=64)
         w2d = keep.tile([P, PASSES, 2 * H], U8, align_bytes=64)
-        w2sd = keep.tile([P, PASSES, H], U8, align_bytes=64)
 
         def deal(dst, src, run):
             nc.vector.tensor_copy(
@@ -92,6 +93,7 @@ def tile_picked_ypdsch_late_p_kernel(tc, x_words, x_scales, w1_words, w1_scales,
         xb0 = keep.tile([P, S], U8, align_bytes=64, tag="xb0")
         nc.vector.tensor_copy(xb0[:], xs[:, 0, :].indirect(offs_sb[:]))
         nc.vector.tensor_copy(xg[:, 0, :], xw[0][:].indirect(offs_sb[:]))
+        w2sd = keep.tile([P, PASSES, H], U8, align_bytes=64, tag="xw0")
         deal(w2sd[:], w2s[:], 16)
         xb1 = keep.tile([P, S], U8, align_bytes=64, tag="w2s")
         nc.vector.tensor_copy(xb1[:], xs[:, 1, :].indirect(offs_sb[:]))
@@ -152,9 +154,9 @@ def tile_picked_ypdsch_late_p_kernel(tc, x_words, x_scales, w1_words, w1_scales,
         def dealt(bank):
             return bank[:].rearrange("p (m t) -> p t m", t=PACK)
 
-        clamped = keep.tile([P, D, PACK, P], F32, tag="clamped_then_logs")
+        clamped = keep.tile([P, D, PACK, P], F32, tag="chain")
         excess = keep.tile([P, D, PACK, P], F32)
-        sig_dc = keep.tile([P, PACK, S], F32)
+        sig_dc = keep.tile([P, PACK, S], F32, tag="sig_dc")
         sig_pf = keep.tile([P, D, PACK, P], F32)
         for t in range(PACK):
             nc.scalar.activation(sig_dc[:, t, :], dc[t][:], ACT.Sigmoid, scale=-1.0)
@@ -169,11 +171,12 @@ def tile_picked_ypdsch_late_p_kernel(tc, x_words, x_scales, w1_words, w1_scales,
         for t in range(PACK):
             nc.vector.tensor_scalar(scaled_slo[:, t, :], slo_sb[:, t, :], unit_sb[:, t : t + 1], None, ALU.mult)
 
-        logs = keep.tile([P, 2, PACK, S], F32, tag="clamped_then_logs")
+        log_dc = keep.tile([P, PACK, S], F32, tag="chain")
         for t in range(PACK):
-            nc.scalar.activation(logs[:, 0, t, :], sig_dc[:, t, :], ACT.Ln, bias=FLOOR)
+            nc.scalar.activation(log_dc[:, t, :], sig_dc[:, t, :], ACT.Ln, bias=FLOOR)
+        log_pf = keep.tile([P, PACK, S], F32, tag="sig_dc")
         for t in range(PACK):
-            nc.scalar.activation(logs[:, 1, t, :].rearrange("p (d m) -> p d m", d=D), sig_pf[:, :, t, :], ACT.Ln)
+            nc.scalar.activation(log_pf[:, t, :].rearrange("p (d m) -> p d m", d=D), sig_pf[:, :, t, :], ACT.Ln)
 
         waits = [psum.tile([P, S], F32, name=f"wait{t}", tag=f"pf{t}") for t in range(PACK)]
         others = [(d, e) for e in range(D) for d in range(D) if e != d]
@@ -182,16 +185,16 @@ def tile_picked_ypdsch_late_p_kernel(tc, x_words, x_scales, w1_words, w1_scales,
                 nc.tensor.matmul(waits[t][:, P * d : P * (d + 1)], excess[:, e, t, :], ident[:], start=(i == 0), stop=False, is_transpose=True)
         for t in range(PACK):
             for i, (d, e) in enumerate(others):
-                nc.tensor.matmul(waits[t][:, P * d : P * (d + 1)], logs[:, 1, t, P * e : P * (e + 1)], ident[:], start=False, stop=(i == len(others) - 1), is_transpose=True)
+                nc.tensor.matmul(waits[t][:, P * d : P * (d + 1)], log_pf[:, t, P * e : P * (e + 1)], ident[:], start=False, stop=(i == len(others) - 1), is_transpose=True)
 
         halves = [(slice(h * HALF, (h + 1) * HALF), pl_sb[:, h * LIST_COLS : (h + 1) * LIST_COLS]) for h in range(2)]
         deco = [keep.tile([P, S], F32, name=f"deco{t}") for t in range(PACK)]
         deco_plus = keep.tile([P, PACK, S], F32)
-        den = keep.tile([P, PACK, S], F32, tag="den_then_rec")
         for t in range(PACK):
-            nc.vector.scalar_tensor_tensor(deco[t][:], logs[:, 0, t, :], -1.0, dc[t][:], ALU.mult, ALU.max)
+            nc.vector.scalar_tensor_tensor(deco[t][:], log_dc[:, t, :], -1.0, dc[t][:], ALU.mult, ALU.max)
             engine = nc.gpsimd if t < PACK - 1 else nc.vector
             engine.tensor_scalar(deco_plus[:, t, :], deco[t][:], 1.0, 0.5, ALU.mult, ALU.add)
+        den = keep.tile([P, PACK, S], F32, tag="chain")
         last = PACK - 1
         den_tail = keep.tile([P, HALF], F32)
         rec_tail = keep.tile([P, HALF], F32)
@@ -205,7 +208,7 @@ def tile_picked_ypdsch_late_p_kernel(tc, x_words, x_scales, w1_words, w1_scales,
         root = keep.tile([P, PACK, S], F32)
         for t, cols in enumerate(by_tables):
             nc.scalar.activation(root[:, t, cols], den[:, t, cols], ACT.Ln, scale=4.0, bias=-1.0)
-        rec = keep.tile([P, PACK, S], F32, tag="den_then_rec")
+        rec = keep.tile([P, PACK, S], F32, tag="chain")
         for t, cols in enumerate(by_tables):
             nc.scalar.activation(rec[:, t, cols], root[:, t, cols], ACT.Sigmoid, scale=-1.0)
 
@@ -214,20 +217,18 @@ def tile_picked_ypdsch_late_p_kernel(tc, x_words, x_scales, w1_words, w1_scales,
         kept = keep.tile([P, PACK, S], F32)
         picked = keep.tile([P, 2, PACK, HALF], F32)
 
-        for step in range(PACK + 2):
-            t = step
-            if t < PACK:
-                cols = by_tables[t]
-                groups = slice(cols.start // D, cols.stop // D)
-                nc.vector.scalar_tensor_tensor(by_group(push[t][:, cols]), in_list_order(waits[t])[:, groups, :], twice_unit[:, t : t + 1], by_group(rec[:, t, cols]), ALU.mult, ALU.mult)
+        def clamp(t):
+            nc.vector.tensor_scalar(kept[:, t, :], room[:, t, :], upper[:, t : t + 1], lower[:, t : t + 1], ALU.min, ALU.max)
+
+        for t, cols in enumerate(by_tables):
+            groups = slice(cols.start // D, cols.stop // D)
+            nc.vector.scalar_tensor_tensor(by_group(push[t][:, cols]), in_list_order(waits[t])[:, groups, :], twice_unit[:, t : t + 1], by_group(rec[:, t, cols]), ALU.mult, ALU.mult)
             if t == last:
                 nc.vector.scalar_tensor_tensor(by_group(push[t][:, HALF:]), in_list_order(waits[t])[:, HALF // D :, :], half_unit[:], by_group(rec_tail[:]), ALU.mult, ALU.mult)
-            t = step - 1
-            if 0 <= t < PACK:
-                nc.vector.scalar_tensor_tensor(room[:, t, :], push[t][:], 2.0, scaled_slo[:, t, :], ALU.mult, ALU.add)
-            t = step - 2
-            if 0 <= t < PACK:
-                nc.vector.tensor_scalar(kept[:, t, :], room[:, t, :], upper[:, t : t + 1], lower[:, t : t + 1], ALU.min, ALU.max)
+            if t > 0:
+                clamp(t - 1)
+            nc.vector.scalar_tensor_tensor(room[:, t, :], push[t][:], 2.0, scaled_slo[:, t, :], ALU.mult, ALU.add)
+        clamp(last)
         for h in range(2):
             for t in range(PACK):
                 nc.scalar.activation(picked[:, h, t, :], push[t][:].indirect(halves[h][1]), ACT.Copy)

@@ -107,15 +107,6 @@ def tile_picked_ypdsch_late_p_kernel(tc, x_words, x_scales, w1_words, w1_scales,
         nc.sync.dma_start(slo_sb[:], slo.rearrange("(p t) s -> p t s", t=PACK))
         load_w_words(w3w, w3_words)
 
-        twice_unit = keep.tile([P, PACK], F32)
-        half_unit = keep.tile([P, 1], F32)
-        upper = keep.tile([P, PACK], F32)
-        lower = keep.tile([P, PACK], F32)
-        nc.vector.tensor_scalar(twice_unit[:], unit_sb[:], 2.0, None, ALU.mult)
-        nc.vector.tensor_scalar(half_unit[:], unit_sb[:, PACK - 1 :], 0.5, None, ALU.mult)
-        nc.vector.tensor_scalar(upper[:], unit_sb[:], 0.0, HUGE, ALU.is_ge, ALU.mult)
-        nc.vector.tensor_scalar(lower[:], unit_sb[:], 0.0, -HUGE, ALU.is_lt, ALU.mult)
-
         dc = [psum.tile([P, S], F32, name=f"dc{t}") for t in range(PACK)]
         pf = [psum.tile([P, H], F32, name=f"pf{d}") for d in range(D)]
         for o in range(PASSES):
@@ -144,6 +135,16 @@ def tile_picked_ypdsch_late_p_kernel(tc, x_words, x_scales, w1_words, w1_scales,
         w3s = keep.tile([P, 1, N], U8, align_bytes=64, tag="xb0")
         nc.vector.memset(w3s[:].bitcast(I32), 0)
         load_scales(nc.sync, w3s, w3_scales)
+
+        per_row = keep.tile([P, 3 * PACK + 1], F32, align_bytes=64, tag="w2s")
+        twice_unit = per_row[:, 0:PACK]
+        upper = per_row[:, PACK : 2 * PACK]
+        lower = per_row[:, 2 * PACK : 3 * PACK]
+        half_unit = per_row[:, 3 * PACK :]
+        nc.vector.tensor_scalar(twice_unit, unit_sb[:], 2.0, None, ALU.mult)
+        nc.vector.tensor_scalar(upper, unit_sb[:], 0.0, HUGE, ALU.is_ge, ALU.mult)
+        nc.vector.tensor_scalar(lower, unit_sb[:], 0.0, -HUGE, ALU.is_lt, ALU.mult)
+        nc.vector.tensor_scalar(half_unit, unit_sb[:, PACK - 1 :], 0.5, None, ALU.mult)
 
         def in_list_order(bank):
             return bank[:].rearrange("p (d v) -> p v d", d=D)
@@ -189,19 +190,23 @@ def tile_picked_ypdsch_late_p_kernel(tc, x_words, x_scales, w1_words, w1_scales,
 
         halves = [(slice(h * HALF, (h + 1) * HALF), pl_sb[:, h * LIST_COLS : (h + 1) * LIST_COLS]) for h in range(2)]
         deco = [keep.tile([P, S], F32, name=f"deco{t}") for t in range(PACK)]
-        deco_plus = keep.tile([P, PACK, S], F32)
+        last = PACK - 1
+        deco_plus = keep.tile([P, last, S], F32)
         for t in range(PACK):
             nc.vector.scalar_tensor_tensor(deco[t][:], log_dc[:, t, :], -1.0, dc[t][:], ALU.mult, ALU.max)
-            engine = nc.gpsimd if t < PACK - 1 else nc.vector
-            engine.tensor_scalar(deco_plus[:, t, :], deco[t][:], 1.0, 0.5, ALU.mult, ALU.add)
+            if t < last:
+                engine = nc.gpsimd if t < 2 else nc.vector
+                engine.tensor_scalar(deco_plus[:, t, :], deco[t][:], 1.0, 0.5, ALU.mult, ALU.add)
         den = keep.tile([P, PACK, S], F32, tag="chain")
-        last = PACK - 1
         den_tail = keep.tile([P, HALF], F32)
         rec_tail = keep.tile([P, HALF], F32)
-        for t in range(PACK):
-            for h, (cols, part) in enumerate(halves):
-                dst = den_tail[:] if (t, h) == (last, 1) else den[:, t, cols]
-                nc.vector.tensor_tensor(dst, deco[t][:].indirect(part), deco_plus[:, t, cols], ALU.add)
+        neighbour = keep.tile([P, S], F32)
+        for t in range(last):
+            for cols, part in halves:
+                nc.vector.tensor_tensor(den[:, t, cols], deco[t][:].indirect(part), deco_plus[:, t, cols], ALU.add)
+        for (cols, part), dst in zip(halves, (den[:, last, :HALF], den_tail[:])):
+            nc.scalar.activation(neighbour[:, cols], deco[last][:].indirect(part), ACT.Copy)
+            nc.vector.scalar_tensor_tensor(dst, neighbour[:, cols], 0.5, deco[last][:, cols], ALU.add, ALU.add)
         nc.vector.reciprocal(rec_tail[:], den_tail[:])
 
         by_tables = [slice(0, S)] * last + [halves[0][0]]
@@ -215,37 +220,44 @@ def tile_picked_ypdsch_late_p_kernel(tc, x_words, x_scales, w1_words, w1_scales,
         push = [keep.tile([P, S], F32, name=f"push{t}") for t in range(PACK)]
         room = keep.tile([P, PACK, S], F32)
         kept = keep.tile([P, PACK, S], F32)
-        picked = keep.tile([P, 2, PACK, HALF], F32)
-
-        def clamp(t):
-            nc.vector.tensor_scalar(kept[:, t, :], room[:, t, :], upper[:, t : t + 1], lower[:, t : t + 1], ALU.min, ALU.max)
-
-        for t, cols in enumerate(by_tables):
-            groups = slice(cols.start // D, cols.stop // D)
-            nc.vector.scalar_tensor_tensor(by_group(push[t][:, cols]), in_list_order(waits[t])[:, groups, :], twice_unit[:, t : t + 1], by_group(rec[:, t, cols]), ALU.mult, ALU.mult)
+        for step in range(PACK + 2):
+            t = step
+            if t < PACK:
+                cols = by_tables[t]
+                groups = slice(cols.start // D, cols.stop // D)
+                nc.vector.scalar_tensor_tensor(by_group(push[t][:, cols]), in_list_order(waits[t])[:, groups, :], twice_unit[:, t : t + 1], by_group(rec[:, t, cols]), ALU.mult, ALU.mult)
             if t == last:
-                nc.vector.scalar_tensor_tensor(by_group(push[t][:, HALF:]), in_list_order(waits[t])[:, HALF // D :, :], half_unit[:], by_group(rec_tail[:]), ALU.mult, ALU.mult)
-            if t > 0:
-                clamp(t - 1)
-            nc.vector.scalar_tensor_tensor(room[:, t, :], push[t][:], 2.0, scaled_slo[:, t, :], ALU.mult, ALU.add)
-        clamp(last)
-        for h in range(2):
-            for t in range(PACK):
-                nc.scalar.activation(picked[:, h, t, :], push[t][:].indirect(halves[h][1]), ACT.Copy)
+                nc.vector.scalar_tensor_tensor(by_group(push[t][:, HALF:]), in_list_order(waits[t])[:, HALF // D :, :], half_unit, by_group(rec_tail[:]), ALU.mult, ALU.mult)
+            t = step - 1
+            if 0 <= t < PACK:
+                nc.vector.scalar_tensor_tensor(room[:, t, :], push[t][:], 2.0, scaled_slo[:, t, :], ALU.mult, ALU.add)
+            t = step - 2
+            if 0 <= t < PACK:
+                nc.vector.tensor_scalar(kept[:, t, :], room[:, t, :], upper[:, t : t + 1], lower[:, t : t + 1], ALU.min, ALU.max)
 
-        for h in range(2):
-            hb = keep.tile([P, HALF, PACK], BF16, name=f"hb{h}", align_bytes=64)
-            codes = keep.tile([P, HALF], U32, name=f"codes{h}", align_bytes=64)
-            hs = keep.tile([P, HALF], U8, name=f"hs{h}", align_bytes=64)
+        parts = [slice(0, 256), slice(256, 384), slice(384, 512)]
+        picked = keep.tile([P, PACK, S], F32)
+        for cols in parts:
+            for t in range(PACK):
+                nc.scalar.activation(picked[:, t, cols], push[t][:].indirect(pl_sb[:, cols.start // 16 : cols.stop // 16]), ACT.Copy)
+
+        rounded = []
+        for h, cols in enumerate(parts):
+            hb = keep.tile([P, cols.stop - cols.start, PACK], BF16, name=f"hb{h}", align_bytes=64)
             nc.vector.tensor_tensor(
                 hb[:].rearrange("p (c i) t -> p c t i", i=4),
-                picked[:, h].rearrange("p t (c i) -> p c t i", i=4),
-                kept[:, :, halves[h][0]].rearrange("p t (c i) -> p c t i", i=4),
+                picked[:, :, cols].rearrange("p t (c i) -> p c t i", i=4),
+                kept[:, :, cols].rearrange("p t (c i) -> p c t i", i=4),
                 ALU.add,
             )
-            nc.vector.quantize_mx(out=codes[:].bitcast(FP8X4), scales=hs[:], in_=hb[:].rearrange("p c t -> p (c t)"))
-            acc = psum.tile([P, HALF], F32, name=f"acc{h}", tag=f"dc{h}")
-            nc.tensor.matmul_mx(out=acc[:], lhsT=w3w[:, 0, :].bitcast(FP4X4), lhsT_scale=w3s[:, 0, :], rhs=codes[:].bitcast(FP8X4), rhs_scale=hs[:], start=True, stop=True)
-            res = keep.tile([P, HALF], F32, name=f"res{h}")
-            nc.scalar.copy(res[:], acc[:])
-            nc.sync.dma_start(out[:, halves[h][0]], res[:])
+            rounded.append(hb)
+            for g in [h - 1] * (h > 0) + [h] * (h == len(parts) - 1):
+                width = parts[g].stop - parts[g].start
+                codes = keep.tile([P, width], U32, name=f"codes{g}", align_bytes=64)
+                hs = keep.tile([P, width], U8, name=f"hs{g}", align_bytes=64)
+                nc.vector.quantize_mx(out=codes[:].bitcast(FP8X4), scales=hs[:], in_=rounded[g][:].rearrange("p c t -> p (c t)"))
+                acc = psum.tile([P, width], F32, name=f"acc{g}", tag=f"dc{g}")
+                nc.tensor.matmul_mx(out=acc[:], lhsT=w3w[:, 0, :].bitcast(FP4X4), lhsT_scale=w3s[:, 0, :], rhs=codes[:].bitcast(FP8X4), rhs_scale=hs[:], start=True, stop=True)
+                res = keep.tile([P, width], F32, name=f"res{g}")
+                nc.scalar.copy(res[:], acc[:])
+                nc.sync.dma_start(out[:, parts[g]], res[:])

from contextlib import ExitStack

import concourse.mybir as mybir
from concourse.masks import make_identity

K, T, S, D, N, H = 1024, 2048, 512, 4, 128, 512
FLOPS = 2 * K * H * S * 2 + 2 * H * N * S

F32 = mybir.dt.float32
BF16 = mybir.dt.bfloat16
I32 = mybir.dt.int32
U32 = mybir.dt.uint32
U16 = mybir.dt.uint16
U8 = mybir.dt.uint8
FP8X4 = mybir.dt.float8_e4m3fn_x4
FP4X4 = mybir.dt.float4_e2m1fn_x4
ACT = mybir.ActivationFunctionType
ALU = mybir.AluOpType

P = 128
PACK = 4
PASSES = K // (P * PACK)
GROUPS = S // D
HALF = S // 2
LIST_COLS = HALF // 16
CLAMP = 32.0
FLOOR = 1.0e-18
HUGE = 3.0e38


def tile_picked_ypdsch_late_p_kernel(tc, x_words, x_scales, w1_words, w1_scales, w2_words, w2_scales, slo, unit, w3_words, w3_scales, offs, pl, out):
    nc = tc.nc
    with ExitStack() as ctx:
        lists = ctx.enter_context(tc.tile_pool(name="lists", bufs=1))
        keep = ctx.enter_context(tc.tile_pool(name="keep", bufs=1))
        psum = ctx.enter_context(tc.psum_pool(name="psum", bufs=1))

        offs_sb = lists.tile([P, S // 16], U16)
        pl_sb = lists.tile([P, S // 16], U16)

        xs = keep.tile([P, PASSES, T], U8, align_bytes=64, tag="xs")
        w2s = keep.tile([P, PASSES, H], U8, align_bytes=64, tag="w2s")
        w1s = keep.tile([P, PASSES, H], U8, align_bytes=64)
        for plane in (xs, w2s, w1s):
            nc.vector.memset(plane[:].bitcast(I32), 0)

        xw = [keep.tile([P, T], U32, name=f"xw{o}", tag=f"xw{o}", align_bytes=64) for o in range(PASSES)]
        w1w = keep.tile([P, PASSES, 2 * H], U8, align_bytes=64)
        w2w = keep.tile([P, PASSES, 2 * H], U8, align_bytes=64, tag="w2w")
        unit_sb = keep.tile([P, PACK], F32)

        def load_scales(queue, dst, src, quadrants=range(4)):
            for q in quadrants:
                queue.dma_start(
                    dst[32 * q : 32 * q + 4].bitcast(I32),
                    src[:, 4 * q : 4 * q + 4, :].rearrange("o r n -> r o n").bitcast(I32),
                )

        def load_x_words(o):
            nc.sync.dma_start(xw[o][:].bitcast(I32), x_words[o].rearrange("p n t -> p (n t)").bitcast(I32))

        def load_w_words(dst, src):
            nc.sync.dma_start(dst[:].bitcast(I32), src.rearrange("o p n -> p o n").bitcast(I32))

        nc.sync.dma_start(offs_sb[:], offs)
        load_scales(nc.sync, xs, x_scales, range(0, 1))
        load_scales(nc.scalar, xs, x_scales, range(1, 4))
        load_w_words(w2w, w2_words)
        load_x_words(0)
        load_scales(nc.sync, w2s, w2_scales, range(0, 2))
        load_scales(nc.scalar, w2s, w2_scales, range(2, 4))
        load_x_words(1)
        nc.sync.dma_start(pl_sb[:], pl)
        load_w_words(w1w, w1_words)
        load_scales(nc.scalar, w1s, w1_scales)
        nc.gpsimd.dma_start(unit_sb[:], unit.rearrange("(p t) o -> p (t o)", t=PACK))

        ident = keep.tile([P, P], F32)
        make_identity(nc, ident[:])

        xg = keep.tile([P, PASSES, S], U32, align_bytes=64)
        xgd = keep.tile([P, PASSES, S], U32, align_bytes=64)
        w2d = keep.tile([P, PASSES, 2 * H], U8, align_bytes=64)

        def deal(dst, src, run):
            nc.vector.tensor_copy(
                dst.rearrange("p o (t c i) -> p o c t i", t=PACK, i=run),
                src.rearrange("p o (c i t) -> p o c t i", t=PACK, i=run),
            )

        deal(w2d[:].bitcast(U16), w2w[:].bitcast(U16), 8)
        w3w = keep.tile([P, 1, 2 * N], U8, align_bytes=64, tag="w2w")
        xb0 = keep.tile([P, S], U8, align_bytes=64, tag="xb0")
        nc.vector.tensor_copy(xb0[:], xs[:, 0, :].indirect(offs_sb[:]))
        nc.vector.tensor_copy(xg[:, 0, :], xw[0][:].indirect(offs_sb[:]))
        w2sd = keep.tile([P, PASSES, H], U8, align_bytes=64, tag="xw0")
        deal(w2sd[:], w2s[:], 16)
        xb1 = keep.tile([P, S], U8, align_bytes=64, tag="w2s")
        nc.vector.tensor_copy(xb1[:], xs[:, 1, :].indirect(offs_sb[:]))
        xb = [xb0, xb1]
        nc.vector.tensor_copy(xg[:, 1, :], xw[1][:].indirect(offs_sb[:]))
        xbd = keep.tile([P, PASSES, S], U8, align_bytes=64, tag="xw1")
        for o in range(PASSES):
            deal(xbd[:, o : o + 1, :], xb[o][:].unsqueeze(1), 16)
        deal(xgd[:], xg[:], 4)
        slo_sb = keep.tile([P, PACK, S], F32, align_bytes=64, tag="xs")
        nc.sync.dma_start(slo_sb[:], slo.rearrange("(p t) s -> p t s", t=PACK))
        load_w_words(w3w, w3_words)

        dc = [psum.tile([P, S], F32, name=f"dc{t}") for t in range(PACK)]
        pf = [psum.tile([P, H], F32, name=f"pf{d}") for d in range(D)]
        for o in range(PASSES):
            for t in range(PACK):
                nc.tensor.matmul_mx(
                    out=dc[t][:],
                    lhsT=w2d[:, o, 2 * P * t : 2 * P * (t + 1)].bitcast(FP4X4),
                    lhsT_scale=w2sd[:, o, P * t : P * (t + 1)],
                    rhs=xg[:, o, :].bitcast(FP8X4),
                    rhs_scale=xb[o][:],
                    start=(o == 0),
                    stop=(o == PASSES - 1),
                )
        for d in range(D):
            for o in range(PASSES):
                nc.tensor.matmul_mx(
                    out=pf[d][:],
                    lhsT=xgd[:, o, P * d : P * (d + 1)].bitcast(FP8X4),
                    lhsT_scale=xbd[:, o, P * d : P * (d + 1)],
                    rhs=w1w[:, o, :].bitcast(FP4X4),
                    rhs_scale=w1s[:, o, :],
                    start=(o == 0),
                    stop=(o == PASSES - 1),
                )

        w3s = keep.tile([P, 1, N], U8, align_bytes=64, tag="xb0")
        nc.vector.memset(w3s[:].bitcast(I32), 0)
        load_scales(nc.sync, w3s, w3_scales)

        per_row = keep.tile([P, 3 * PACK + 1], F32, align_bytes=64, tag="w2s")
        twice_unit = per_row[:, 0:PACK]
        upper = per_row[:, PACK : 2 * PACK]
        lower = per_row[:, 2 * PACK : 3 * PACK]
        half_unit = per_row[:, 3 * PACK :]
        nc.vector.tensor_scalar(twice_unit, unit_sb[:], 2.0, None, ALU.mult)
        nc.vector.tensor_scalar(upper, unit_sb[:], 0.0, HUGE, ALU.is_ge, ALU.mult)
        nc.vector.tensor_scalar(lower, unit_sb[:], 0.0, -HUGE, ALU.is_lt, ALU.mult)
        nc.vector.tensor_scalar(half_unit, unit_sb[:, PACK - 1 :], 0.5, None, ALU.mult)

        def in_list_order(bank):
            return bank[:].rearrange("p (d v) -> p v d", d=D)

        def by_group(rows):
            return rows.rearrange("p (v d) -> p v d", d=D)

        def dealt(bank):
            return bank[:].rearrange("p (m t) -> p t m", t=PACK)

        clamped = keep.tile([P, D, PACK, P], F32, tag="chain")
        excess = keep.tile([P, D, PACK, P], F32)
        sig_dc = keep.tile([P, PACK, S], F32, tag="sig_dc")
        sig_pf = keep.tile([P, D, PACK, P], F32)
        for t in range(PACK):
            nc.scalar.activation(sig_dc[:, t, :], dc[t][:], ACT.Sigmoid, scale=-1.0)
        for d in range(D):
            nc.vector.tensor_scalar(clamped[:, d], dealt(pf[d]), CLAMP, None, ALU.min)
        for d in range(D):
            nc.scalar.activation(sig_pf[:, d], clamped[:, d], ACT.Sigmoid, scale=-1.0)
        for d in range(D):
            nc.vector.tensor_tensor(excess[:, d], clamped[:, d], dealt(pf[d]), ALU.subtract)

        scaled_slo = keep.tile([P, PACK, S], F32)
        for t in range(PACK):
            nc.vector.tensor_scalar(scaled_slo[:, t, :], slo_sb[:, t, :], unit_sb[:, t : t + 1], None, ALU.mult)

        log_dc = keep.tile([P, PACK, S], F32, tag="chain")
        for t in range(PACK):
            nc.scalar.activation(log_dc[:, t, :], sig_dc[:, t, :], ACT.Ln, bias=FLOOR)
        log_pf = keep.tile([P, PACK, S], F32, tag="sig_dc")
        for t in range(PACK):
            nc.scalar.activation(log_pf[:, t, :].rearrange("p (d m) -> p d m", d=D), sig_pf[:, :, t, :], ACT.Ln)

        waits = [psum.tile([P, S], F32, name=f"wait{t}", tag=f"pf{t}") for t in range(PACK)]
        others = [(d, e) for e in range(D) for d in range(D) if e != d]
        for t in range(PACK):
            for i, (d, e) in enumerate(others):
                nc.tensor.matmul(waits[t][:, P * d : P * (d + 1)], excess[:, e, t, :], ident[:], start=(i == 0), stop=False, is_transpose=True)
        for t in range(PACK):
            for i, (d, e) in enumerate(others):
                nc.tensor.matmul(waits[t][:, P * d : P * (d + 1)], log_pf[:, t, P * e : P * (e + 1)], ident[:], start=False, stop=(i == len(others) - 1), is_transpose=True)

        halves = [(slice(h * HALF, (h + 1) * HALF), pl_sb[:, h * LIST_COLS : (h + 1) * LIST_COLS]) for h in range(2)]
        deco = [keep.tile([P, S], F32, name=f"deco{t}") for t in range(PACK)]
        last = PACK - 1
        deco_plus = keep.tile([P, last, S], F32)
        for t in range(PACK):
            nc.vector.scalar_tensor_tensor(deco[t][:], log_dc[:, t, :], -1.0, dc[t][:], ALU.mult, ALU.max)
            if t < last:
                engine = nc.gpsimd if t < 2 else nc.vector
                engine.tensor_scalar(deco_plus[:, t, :], deco[t][:], 1.0, 0.5, ALU.mult, ALU.add)
        den = keep.tile([P, PACK, S], F32, tag="chain")
        den_tail = keep.tile([P, HALF], F32)
        rec_tail = keep.tile([P, HALF], F32)
        neighbour = keep.tile([P, S], F32)
        for t in range(last):
            for cols, part in halves:
                nc.vector.tensor_tensor(den[:, t, cols], deco[t][:].indirect(part), deco_plus[:, t, cols], ALU.add)
        for (cols, part), dst in zip(halves, (den[:, last, :HALF], den_tail[:])):
            nc.scalar.activation(neighbour[:, cols], deco[last][:].indirect(part), ACT.Copy)
            nc.vector.scalar_tensor_tensor(dst, neighbour[:, cols], 0.5, deco[last][:, cols], ALU.add, ALU.add)
        nc.vector.reciprocal(rec_tail[:], den_tail[:])

        by_tables = [slice(0, S)] * last + [halves[0][0]]
        root = keep.tile([P, PACK, S], F32)
        for t, cols in enumerate(by_tables):
            nc.scalar.activation(root[:, t, cols], den[:, t, cols], ACT.Ln, scale=4.0, bias=-1.0)
        rec = keep.tile([P, PACK, S], F32, tag="chain")
        for t, cols in enumerate(by_tables):
            nc.scalar.activation(rec[:, t, cols], root[:, t, cols], ACT.Sigmoid, scale=-1.0)

        push = [keep.tile([P, S], F32, name=f"push{t}") for t in range(PACK)]
        room = keep.tile([P, PACK, S], F32)
        kept = keep.tile([P, PACK, S], F32)
        for step in range(PACK + 2):
            t = step
            if t < PACK:
                cols = by_tables[t]
                groups = slice(cols.start // D, cols.stop // D)
                nc.vector.scalar_tensor_tensor(by_group(push[t][:, cols]), in_list_order(waits[t])[:, groups, :], twice_unit[:, t : t + 1], by_group(rec[:, t, cols]), ALU.mult, ALU.mult)
            if t == last:
                nc.vector.scalar_tensor_tensor(by_group(push[t][:, HALF:]), in_list_order(waits[t])[:, HALF // D :, :], half_unit, by_group(rec_tail[:]), ALU.mult, ALU.mult)
            t = step - 1
            if 0 <= t < PACK:
                nc.vector.scalar_tensor_tensor(room[:, t, :], push[t][:], 2.0, scaled_slo[:, t, :], ALU.mult, ALU.add)
            t = step - 2
            if 0 <= t < PACK:
                nc.vector.tensor_scalar(kept[:, t, :], room[:, t, :], upper[:, t : t + 1], lower[:, t : t + 1], ALU.min, ALU.max)

        parts = [slice(0, 256), slice(256, 384), slice(384, 512)]
        picked = keep.tile([P, PACK, S], F32)
        for cols in parts:
            for t in range(PACK):
                nc.scalar.activation(picked[:, t, cols], push[t][:].indirect(pl_sb[:, cols.start // 16 : cols.stop // 16]), ACT.Copy)

        rounded = []
        for h, cols in enumerate(parts):
            hb = keep.tile([P, cols.stop - cols.start, PACK], BF16, name=f"hb{h}", align_bytes=64)
            nc.vector.tensor_tensor(
                hb[:].rearrange("p (c i) t -> p c t i", i=4),
                picked[:, :, cols].rearrange("p t (c i) -> p c t i", i=4),
                kept[:, :, cols].rearrange("p t (c i) -> p c t i", i=4),
                ALU.add,
            )
            rounded.append(hb)
            for g in [h - 1] * (h > 0) + [h] * (h == len(parts) - 1):
                width = parts[g].stop - parts[g].start
                codes = keep.tile([P, width], U32, name=f"codes{g}", align_bytes=64)
                hs = keep.tile([P, width], U8, name=f"hs{g}", align_bytes=64)
                nc.vector.quantize_mx(out=codes[:].bitcast(FP8X4), scales=hs[:], in_=rounded[g][:].rearrange("p c t -> p (c t)"))
                acc = psum.tile([P, width], F32, name=f"acc{g}", tag=f"dc{g}")
                nc.tensor.matmul_mx(out=acc[:], lhsT=w3w[:, 0, :].bitcast(FP4X4), lhsT_scale=w3s[:, 0, :], rhs=codes[:].bitcast(FP8X4), rhs_scale=hs[:], start=True, stop=True)
                res = keep.tile([P, width], F32, name=f"res{g}")
                nc.scalar.copy(res[:], acc[:])
                nc.sync.dma_start(out[:, parts[g]], res[:])
